import numpy as np
import ml_dtypes


def mxq(x, axis, fmt="e4m3"):
    dtype, down = {"e4m3": (ml_dtypes.float8_e4m3fn, 7), "e5m2": (ml_dtypes.float8_e5m2, 14)}[fmt]
    v = np.moveaxis(np.asarray(x, np.float32).astype(ml_dtypes.bfloat16).astype(np.float64), axis, -1)
    blocks = v.reshape(v.shape[:-1] + (-1, 32))
    amax = np.abs(blocks).max(-1, keepdims=True)
    byte = np.maximum(np.where(amax > 0, np.frexp(amax)[1] - 1 + 127, 0) - down, 1)
    scale = np.exp2(byte - 127.0)
    codes = (blocks / scale).astype(np.float32).astype(dtype).astype(np.float64)
    return np.moveaxis((codes * scale).reshape(v.shape), -1, axis)


WIDE = False


def mx_kscale(k):
    if not WIDE:
        return np.ones(k)
    levels = np.array([10, -10, 5, -5, 0])
    if k % 512:
        return np.exp2(np.random.permutation(np.resize(levels, k // 32))).repeat(32)
    a = np.empty((k // 512, 16))
    for p in range(k // 512):
        a[p, :8] = np.random.permutation(np.resize(levels, 8))
        for g in range(8):
            far = levels[np.abs(levels - a[p, g]) >= 10]
            a[p, g + 8] = far[np.random.randint(len(far))]
    return np.exp2(a.ravel()).repeat(32)


def f64(x):
    return np.asarray(x).astype(np.float64)


def striped(idx):
    return np.tile(np.asarray(idx).reshape(-1, 16).T, (8, 1)).astype(np.uint16)


def unstriped(offs):
    return offs[:16].T.reshape(-1).astype(np.int64)


E2M1 = np.array([0.0, 0.5, 1.0, 1.5, 2.0, 3.0, 4.0, 6.0, -0.0, -0.5, -1.0, -1.5, -2.0, -3.0, -4.0, -6.0])


def pack_weight(w, fmt):
    k, n = w.shape
    w = f64(np.asarray(w, np.float32).astype(ml_dtypes.bfloat16)).reshape(k // 32, 32, n)
    amax = np.abs(w).max(1)
    if fmt == "e4m3":
        byte = np.frexp(amax)[1] - 1 + 127 - 7
    else:
        mant, ex = np.frexp(amax / 6.0)
        byte = np.where(mant > 0.5, ex, ex - 1) + 127
    byte = np.clip(np.where(amax > 0, byte, 1), 1, 254)
    scaled = (w * np.exp2(127.0 - byte)[:, None, :]).reshape(k, n).astype(np.float32)
    by_word = np.ascontiguousarray(scaled.reshape(k // 512, 128, 4, n).transpose(0, 1, 3, 2))
    if fmt == "e4m3":
        words = by_word.astype(ml_dtypes.float8_e4m3fn).view(np.uint8)
    else:
        c = by_word.astype(ml_dtypes.float4_e2m1fn).view(np.uint8) & 0xF
        words = (c[..., 0::2] | (c[..., 1::2] << 4)).reshape(k // 512, 128, 2 * n)
    return np.ascontiguousarray(words), np.ascontiguousarray(byte.astype(np.uint8).reshape(k // 512, 16, n))


def unpack_weight(words, scales, fmt):
    g, _, n = scales.shape
    words = np.ascontiguousarray(words).reshape(g, 128, n, -1)
    if fmt == "e4m3":
        vals = words.view(ml_dtypes.float8_e4m3fn).astype(np.float64)
    else:
        nib = np.empty((g, 128, n, 4), np.uint8)
        nib[..., 0::2] = words & 0xF
        nib[..., 1::2] = words >> 4
        vals = E2M1[nib]
    vals = vals * np.repeat(np.exp2(scales.astype(np.float64) - 127.0), 8, axis=1)[..., None]
    return vals.transpose(0, 1, 3, 2).reshape(g * 512, n)


def sigmoid(v):
    return 1.0 / (1.0 + np.exp(-v))


D, T, I, Q, E, U, M = 512, 2048, 512, 512, 512, 1024, 1024


def setup_inputs():
    n = np.random.standard_normal
    idx = np.random.permutation(T)[:I]
    idx2 = np.random.permutation(U)[:Q]
    idx3 = np.random.permutation(U)[:Q]
    idx4 = np.random.permutation(M)[:I]
    fd = mx_kscale(D)
    fq = mx_kscale(Q)
    keysp = pack_weight(n((D, T)) / fd[:, None], "e2m1")
    return {
        "users": (n((D, U)) * 1.0 / np.sqrt(D) * fd[:, None]).astype(np.float32),
        "keys_words": keysp[0],
        "keys_scales": keysp[1],
        "qs": (np.random.uniform(0.5, 2.0, (Q, 1)) * fq[:, None]).astype(np.float32),
        "msgs": (n((Q, E)) * 1 / np.sqrt(Q) / fq[:, None]).astype(np.float32),
        "old": (n((E, M)) * 1.0).astype(np.float32),
        "fade": (np.random.uniform(0.3, 0.9, (1, M))).astype(np.float32),
        "offs": striped(idx),
        "offs2": striped(idx2),
        "offs3": striped(idx3),
        "offs4": striped(idx4),
    }


def reference(users, keys_words, keys_scales, qs, msgs, old, fade, offs, offs2, offs3, offs4):
    idx = unstriped(offs)
    idx2 = unstriped(offs2)
    idx3 = unstriped(offs3)
    idx4 = unstriped(offs4)
    keysu = unpack_weight(keys_words, keys_scales, "e2m1")
    zq = np.maximum(f64(users)[:, idx2], f64(users)[:, idx3])
    zqq = mxq(zq, 0, "e4m3")
    keysidxg = keysu[:, idx]
    s = zqq.T @ keysidxg
    w = sigmoid(s)
    wq = w * f64(qs)
    msgsq = mxq(f64(msgs), 0, "e4m3")
    wqq = mxq(wq, 0, "e4m3")
    dl = msgsq.T @ wqq
    df = np.zeros((E, M))
    df[:, idx4] = dl
    y = f64(old) * f64(fade) + df
    return y

@@ -1,0 +1,218 @@
+from contextlib import ExitStack
+
+import concourse.mybir as mybir
+from concourse.masks import make_identity
+
+D, T, I, Q, E, U, M = 512, 2048, 512, 512, 512, 1024, 1024
+FLOPS = 2 * D * Q * I + 2 * Q * E * I
+
+F32 = mybir.dt.float32
+BF16 = mybir.dt.bfloat16
+I32 = mybir.dt.int32
+U32 = mybir.dt.uint32
+U16 = mybir.dt.uint16
+U8 = mybir.dt.uint8
+FP8X4 = mybir.dt.float8_e4m3fn_x4
+FP4X4 = mybir.dt.float4_e2m1fn_x4
+ALU = mybir.AluOpType
+ACT = mybir.ActivationFunctionType
+
+P = 128
+PACK = 4
+BANK = 512
+CHUNK = 128
+HALF = 256
+LIST_COLS = 32
+
+
+def tile_attend_querylarger_delivered_lean_kernel(
+    tc, users, keys_words, keys_scales, qs, msgs, old, fade, offs, offs2, offs3, offs4, out
+):
+    nc = tc.nc
+    with ExitStack() as ctx:
+        keep = ctx.enter_context(tc.tile_pool(name="keep", bufs=1))
+        psum = ctx.enter_context(tc.psum_pool(name="psum", bufs=1))
+
+        def gather(on_vector, dst, window, offsets):
+            if on_vector:
+                nc.vector.tensor_copy(dst, window.indirect(offsets))
+            else:
+                nc.scalar.activation(dst, window.indirect(offsets), ACT.Copy)
+
+        def scatter(on_vector, window, offsets, src):
+            if on_vector:
+                nc.vector.tensor_copy(window.indirect(offsets), src)
+            else:
+                nc.scalar.activation(window.indirect(offsets), src, ACT.Copy)
+
+        token_list = keep.tile([P, LIST_COLS], U16, name="token_list")
+        first_list = keep.tile([P, LIST_COLS], U16, name="first_list")
+        second_list = keep.tile([P, LIST_COLS], U16, name="second_list")
+        place_list = keep.tile([P, LIST_COLS], U16, name="place_list")
+        key_words = keep.tile([P, T], U16, name="key_words")
+        key_bytes = keep.tile([P, T], U8, name="key_bytes")
+        planes = [keep.tile([P, U], F32, name=f"plane{t}") for t in range(PACK)]
+        msgs_raw = keep.tile([P, PACK, E], F32, name="msgs_raw")
+        qs_sb = keep.tile([P, P], F32, name="qs_sb")
+        fade_sb = keep.tile([P, 2, PACK], F32, name="fade_sb")
+        olds = [keep.tile([P, M], F32, name=f"old{j}") for j in range(PACK)]
+        placed = [keep.tile([P, M], F32, name=f"placed{j}") for j in range(PACK)]
+        ident = keep.tile([P, P], F32, name="ident")
+
+        nc.vector.memset(key_bytes[:].bitcast(I32), 0)
+        nc.vector.memset(qs_sb[:], 0.0)
+        users_v = users.rearrange("(p t) u -> p t u", t=PACK)
+        nc.sync.dma_start(first_list[:], offs2)
+        nc.sync.dma_start(planes[0][:], users_v[:, 0, :])
+        nc.sync.dma_start(token_list[:], offs)
+        for g in range(4):
+            nc.sync.dma_start(
+                key_bytes[32 * g : 32 * g + 4, :].bitcast(I32), keys_scales[0, 4 * g : 4 * g + 4, :].bitcast(I32)
+            )
+        nc.sync.dma_start(key_words[:].bitcast(I32), keys_words[0].bitcast(I32))
+        nc.sync.dma_start(second_list[:], offs3)
+        for t in range(1, PACK):
+            nc.sync.dma_start(planes[t][:], users_v[:, t, :])
+        nc.sync.dma_start(fade_sb[:], fade.rearrange("o (h p b) -> p (o h) b", h=2, b=PACK))
+        nc.sync.dma_start(qs_sb[:, 0:PACK], qs.rearrange("(p r) o -> p (r o)", r=PACK))
+        nc.sync.dma_start(msgs_raw[:], msgs.rearrange("(p r) e -> p r e", r=PACK))
+        nc.sync.dma_start(place_list[:], offs4)
+        for j in range(PACK):
+            nc.sync.dma_start(olds[j][:], old[P * j : P * (j + 1), :])
+        make_identity(nc, ident[:])
+        for j in range(PACK):
+            nc.gpsimd.memset(placed[j][:], 0.0)
+
+        first = keep.tile([P, PACK, Q], F32, name="first")
+        second = keep.tile([P, PACK, Q], F32, name="second")
+        got_words = keep.tile([P, I], U16, name="got_words", align_bytes=64)
+        got_bytes = keep.tile([P, I], U8, name="got_bytes", align_bytes=64)
+        gather(False, first[:, 0, :], planes[0][:], first_list[:])
+        nc.vector.tensor_copy(got_bytes[:], key_bytes[:].indirect(token_list[:]))
+        nc.vector.tensor_copy(got_words[:], key_words[:].indirect(token_list[:]))
+        gather(False, second[:, 0, :], planes[0][:], second_list[:])
+        for t in range(1, PACK - 1):
+            gather(True, first[:, t, :], planes[t][:], first_list[:])
+            gather(False, second[:, t, :], planes[t][:], second_list[:])
+
+        zq = keep.tile([P, PACK, P, PACK], BF16, name="zq", tag="zq_then_faded", align_bytes=64)
+        last = PACK - 1
+        for c in range(4):
+            rows = slice(c * CHUNK, (c + 1) * CHUNK)
+            entries = slice(c * 8, (c + 1) * 8)
+            gather(c == 0, first[:, last, rows], planes[last][:], first_list[:, entries])
+            gather(False, second[:, last, rows], planes[last][:], second_list[:, entries])
+            nc.vector.tensor_tensor(
+                zq[:, :, c * 32 : (c + 1) * 32, :].rearrange("p r s t -> p s t r"),
+                first[:, :, rows].rearrange("p t (s r) -> p s t r", r=PACK),
+                second[:, :, rows].rearrange("p t (s r) -> p s t r", r=PACK),
+                ALU.max,
+            )
+        zq_codes = keep.tile([P, Q], U32, name="zq_codes", align_bytes=64)
+        zq_scales = keep.tile([P, Q], U8, name="zq_scales", align_bytes=64)
+        nc.vector.quantize_mx(zq_codes[:].bitcast(FP8X4), zq_scales[:], zq[:].rearrange("p r s t -> p (r s t)"))
+
+        fade_all = keep.tile([P, M], F32, name="fade_all")
+        for h in range(2):
+            fade_ps = psum.tile([P, PACK, P], F32, name=f"fade_ps{h}")
+            for b in range(PACK):
+                nc.tensor.transpose(fade_ps[:, b, :], fade_sb[:, h, b : b + 1].to_broadcast([P, P]), ident[:])
+            nc.scalar.copy(
+                fade_all[:, h * BANK : (h + 1) * BANK].rearrange("p (n b) -> p n b", b=PACK),
+                fade_ps[:].rearrange("p b n -> p n b"),
+            )
+        qs_ps = psum.tile([P, 2, P], F32, name="qs_ps")
+        qs_turned = keep.tile([P, P], F32, name="qs_turned")
+        nc.tensor.transpose(qs_ps[:, 0, :], qs_sb[:], ident[:])
+        nc.scalar.copy(qs_turned[:], qs_ps[:, 0, :])
+        nc.tensor.transpose(qs_ps[:, 1, :], qs_turned[:], ident[:])
+
+        msgs_codes = keep.tile([P, E], U32, name="msgs_codes", align_bytes=64)
+        msgs_scales = keep.tile([P, E], U8, name="msgs_scales", align_bytes=64)
+        for h in range(2):
+            cols = slice(h * HALF, (h + 1) * HALF)
+            msgs_bf = keep.tile([P, HALF, PACK], BF16, name=f"msgs_bf{h}", align_bytes=64)
+            dst = msgs_bf[:].rearrange("p (c i) r -> p c r i", i=4)
+            src = msgs_raw[:, :, cols].rearrange("p r (c i) -> p c r i", i=4)
+            if h == 0:
+                nc.vector.tensor_copy(dst, src)
+            else:
+                nc.scalar.copy(dst, src)
+            nc.vector.quantize_mx(
+                msgs_codes[:, cols].bitcast(FP8X4), msgs_scales[:, cols], msgs_bf[:].rearrange("p e r -> p (e r)")
+            )
+
+        faded = [keep.tile([P, M], F32, name="faded0", tag="zq_then_faded", align_bytes=64)]
+        faded.extend(keep.tile([P, M], F32, name=f"faded{j}") for j in range(1, PACK))
+        for j in range(PACK):
+            for c in range(4):
+                cols = slice(c * HALF, (c + 1) * HALF)
+                nc.gpsimd.tensor_tensor(faded[j][:, cols], olds[j][:, cols], fade_all[:, cols], ALU.mult)
+
+        dl_early = keep.tile([P, PACK, 3 * CHUNK], F32, name="dl_early")
+        dl_late = keep.tile([P, PACK, CHUNK], F32, name="dl_late")
+        wqs = []
+
+        def weigh(c):
+            cols = slice(c * CHUNK, (c + 1) * CHUNK)
+            scores = psum.tile([P, PACK, CHUNK], F32, name="scores", bufs=2)
+            for r in range(PACK):
+                nc.tensor.matmul_mx(
+                    scores[:, r, :],
+                    lhsT=zq_codes[:, r * P : (r + 1) * P].bitcast(FP8X4),
+                    lhsT_scale=zq_scales[:, r * P : (r + 1) * P],
+                    rhs=got_words[:, cols].bitcast(FP4X4),
+                    rhs_scale=got_bytes[:, cols],
+                    start=True,
+                    stop=True,
+                )
+            w = keep.tile([P, CHUNK, PACK], F32, name=f"w{c}")
+            nc.scalar.activation(w[:], scores[:].rearrange("p r n -> p n r"), ACT.Sigmoid)
+            wq = keep.tile([P, CHUNK, PACK], BF16, name=f"wq{c}", align_bytes=64)
+            nc.vector.tensor_tensor(
+                wq[:], w[:], qs_ps[:, 1, 0:PACK].unsqueeze(1).to_broadcast([P, CHUNK, PACK]), ALU.mult
+            )
+            wqs.append(wq)
+
+        def carry(c):
+            wq_codes = keep.tile([P, CHUNK], U32, name=f"wq_codes{c}", align_bytes=64)
+            wq_scales = keep.tile([P, CHUNK], U8, name=f"wq_scales{c}", align_bytes=64)
+            nc.vector.quantize_mx(wq_codes[:].bitcast(FP8X4), wq_scales[:], wqs[c][:].rearrange("p n r -> p (n r)"))
+            acc = psum.tile([P, PACK, CHUNK], F32, name="acc", bufs=3)
+            for j in range(PACK):
+                nc.tensor.matmul_mx(
+                    acc[:, j, :],
+                    lhsT=msgs_codes[:, j * P : (j + 1) * P].bitcast(FP8X4),
+                    lhsT_scale=msgs_scales[:, j * P : (j + 1) * P],
+                    rhs=wq_codes[:].bitcast(FP8X4),
+                    rhs_scale=wq_scales[:],
+                    start=True,
+                    stop=True,
+                )
+            nc.scalar.copy(dl_early[:, :, c * CHUNK : (c + 1) * CHUNK] if c < 3 else dl_late[:], acc[:])
+
+        weigh(0)
+        for c in range(1, 4):
+            weigh(c)
+            carry(c - 1)
+        carry(3)
+
+        def place_early(on_vector, j):
+            scatter(on_vector, placed[j][:], place_list[:, 0:24], dl_early[:, j, :])
+
+        def place_late(on_vector, j):
+            scatter(on_vector, placed[j][:], place_list[:, 24:32], dl_late[:, j, :])
+
+        place_early(True, 2)
+        place_late(False, 1)
+        place_early(False, 1)
+        place_early(True, 0)
+        place_late(True, 0)
+        place_late(False, 2)
+        place_late(False, 3)
+        place_early(False, 3)
+        for j in (1, 0, 2, 3):
+            edges = (0, 512, 1024) if j < 3 else (0, 512, 768, 1024)
+            for lo, hi in zip(edges, edges[1:]):
+                nc.vector.tensor_tensor(faded[j][:, lo:hi], faded[j][:, lo:hi], placed[j][:, lo:hi], ALU.add)
+                nc.sync.dma_start(out[P * j : P * (j + 1), lo:hi], faded[j][:, lo:hi])

@@ -61,6 +61,8 @@ def tile_attend_querylarger_delivered_lean_kernel(
 
         nc.vector.memset(key_bytes[:].bitcast(I32), 0)
         nc.vector.memset(qs_sb[:], 0.0)
+        warm = keep.tile([P, 1], F32, name="warm")
+        nc.scalar.activation(warm[:], qs_sb[:, P - 1 : P], ACT.Sigmoid)
         users_v = users.rearrange("(p t) u -> p t u", t=PACK)
         nc.sync.dma_start(first_list[:], offs2)
         nc.sync.dma_start(planes[0][:], users_v[:, 0, :])

from contextlib import ExitStack

import concourse.mybir as mybir
from concourse.masks import make_identity

D, T, I, Q, E, U, M = 512, 2048, 512, 512, 512, 1024, 1024
FLOPS = 2 * D * Q * I + 2 * Q * E * I

F32 = mybir.dt.float32
BF16 = mybir.dt.bfloat16
I32 = mybir.dt.int32
U32 = mybir.dt.uint32
U16 = mybir.dt.uint16
U8 = mybir.dt.uint8
FP8X4 = mybir.dt.float8_e4m3fn_x4
FP4X4 = mybir.dt.float4_e2m1fn_x4
ALU = mybir.AluOpType
ACT = mybir.ActivationFunctionType

P = 128
PACK = 4
BANK = 512
CHUNK = 128
HALF = 256
LIST_COLS = 32


def tile_attend_querylarger_delivered_lean_kernel(
    tc, users, keys_words, keys_scales, qs, msgs, old, fade, offs, offs2, offs3, offs4, out
):
    nc = tc.nc
    with ExitStack() as ctx:
        keep = ctx.enter_context(tc.tile_pool(name="keep", bufs=1))
        psum = ctx.enter_context(tc.psum_pool(name="psum", bufs=1))

        def gather(on_vector, dst, window, offsets):
            if on_vector:
                nc.vector.tensor_copy(dst, window.indirect(offsets))
            else:
                nc.scalar.activation(dst, window.indirect(offsets), ACT.Copy)

        def scatter(on_vector, window, offsets, src):
            if on_vector:
                nc.vector.tensor_copy(window.indirect(offsets), src)
            else:
                nc.scalar.activation(window.indirect(offsets), src, ACT.Copy)

        token_list = keep.tile([P, LIST_COLS], U16, name="token_list")
        first_list = keep.tile([P, LIST_COLS], U16, name="first_list")
        second_list = keep.tile([P, LIST_COLS], U16, name="second_list")
        place_list = keep.tile([P, LIST_COLS], U16, name="place_list")
        key_words = keep.tile([P, T], U16, name="key_words")
        key_bytes = keep.tile([P, T], U8, name="key_bytes")
        planes = [keep.tile([P, U], F32, name=f"plane{t}") for t in range(PACK)]
        msgs_raw = keep.tile([P, PACK, E], F32, name="msgs_raw")
        qs_sb = keep.tile([P, P], F32, name="qs_sb")
        fade_sb = keep.tile([P, 2, PACK], F32, name="fade_sb")
        olds = [keep.tile([P, M], F32, name=f"old{j}") for j in range(PACK)]
        placed = [keep.tile([P, M], F32, name=f"placed{j}") for j in range(PACK)]
        ident = keep.tile([P, P], F32, name="ident")

        nc.vector.memset(key_bytes[:].bitcast(I32), 0)
        nc.vector.memset(qs_sb[:], 0.0)
        warm = keep.tile([P, 1], F32, name="warm")
        nc.scalar.activation(warm[:], qs_sb[:, P - 1 : P], ACT.Sigmoid)
        users_v = users.rearrange("(p t) u -> p t u", t=PACK)
        nc.sync.dma_start(first_list[:], offs2)
        nc.sync.dma_start(planes[0][:], users_v[:, 0, :])
        nc.sync.dma_start(token_list[:], offs)
        for g in range(4):
            nc.sync.dma_start(
                key_bytes[32 * g : 32 * g + 4, :].bitcast(I32), keys_scales[0, 4 * g : 4 * g + 4, :].bitcast(I32)
            )
        nc.sync.dma_start(key_words[:].bitcast(I32), keys_words[0].bitcast(I32))
        nc.sync.dma_start(second_list[:], offs3)
        for t in range(1, PACK):
            nc.sync.dma_start(planes[t][:], users_v[:, t, :])
        nc.sync.dma_start(fade_sb[:], fade.rearrange("o (h p b) -> p (o h) b", h=2, b=PACK))
        nc.sync.dma_start(qs_sb[:, 0:PACK], qs.rearrange("(p r) o -> p (r o)", r=PACK))
        nc.sync.dma_start(msgs_raw[:], msgs.rearrange("(p r) e -> p r e", r=PACK))
        nc.sync.dma_start(place_list[:], offs4)
        for j in range(PACK):
            nc.sync.dma_start(olds[j][:], old[P * j : P * (j + 1), :])
        make_identity(nc, ident[:])
        for j in range(PACK):
            nc.gpsimd.memset(placed[j][:], 0.0)

        first = keep.tile([P, PACK, Q], F32, name="first")
        second = keep.tile([P, PACK, Q], F32, name="second")
        got_words = keep.tile([P, I], U16, name="got_words", align_bytes=64)
        got_bytes = keep.tile([P, I], U8, name="got_bytes", align_bytes=64)
        gather(False, first[:, 0, :], planes[0][:], first_list[:])
        nc.vector.tensor_copy(got_bytes[:], key_bytes[:].indirect(token_list[:]))
        nc.vector.tensor_copy(got_words[:], key_words[:].indirect(token_list[:]))
        gather(False, second[:, 0, :], planes[0][:], second_list[:])
        for t in range(1, PACK - 1):
            gather(True, first[:, t, :], planes[t][:], first_list[:])
            gather(False, second[:, t, :], planes[t][:], second_list[:])

        zq = keep.tile([P, PACK, P, PACK], BF16, name="zq", tag="zq_then_faded", align_bytes=64)
        last = PACK - 1
        for c in range(4):
            rows = slice(c * CHUNK, (c + 1) * CHUNK)
            entries = slice(c * 8, (c + 1) * 8)
            gather(c == 0, first[:, last, rows], planes[last][:], first_list[:, entries])
            gather(False, second[:, last, rows], planes[last][:], second_list[:, entries])
            nc.vector.tensor_tensor(
                zq[:, :, c * 32 : (c + 1) * 32, :].rearrange("p r s t -> p s t r"),
                first[:, :, rows].rearrange("p t (s r) -> p s t r", r=PACK),
                second[:, :, rows].rearrange("p t (s r) -> p s t r", r=PACK),
                ALU.max,
            )
        zq_codes = keep.tile([P, Q], U32, name="zq_codes", align_bytes=64)
        zq_scales = keep.tile([P, Q], U8, name="zq_scales", align_bytes=64)
        nc.vector.quantize_mx(zq_codes[:].bitcast(FP8X4), zq_scales[:], zq[:].rearrange("p r s t -> p (r s t)"))

        fade_all = keep.tile([P, M], F32, name="fade_all")
        for h in range(2):
            fade_ps = psum.tile([P, PACK, P], F32, name=f"fade_ps{h}")
            for b in range(PACK):
                nc.tensor.transpose(fade_ps[:, b, :], fade_sb[:, h, b : b + 1].to_broadcast([P, P]), ident[:])
            nc.scalar.copy(
                fade_all[:, h * BANK : (h + 1) * BANK].rearrange("p (n b) -> p n b", b=PACK),
                fade_ps[:].rearrange("p b n -> p n b"),
            )
        qs_ps = psum.tile([P, 2, P], F32, name="qs_ps")
        qs_turned = keep.tile([P, P], F32, name="qs_turned")
        nc.tensor.transpose(qs_ps[:, 0, :], qs_sb[:], ident[:])
        nc.scalar.copy(qs_turned[:], qs_ps[:, 0, :])
        nc.tensor.transpose(qs_ps[:, 1, :], qs_turned[:], ident[:])

        msgs_codes = keep.tile([P, E], U32, name="msgs_codes", align_bytes=64)
        msgs_scales = keep.tile([P, E], U8, name="msgs_scales", align_bytes=64)
        for h in range(2):
            cols = slice(h * HALF, (h + 1) * HALF)
            msgs_bf = keep.tile([P, HALF, PACK], BF16, name=f"msgs_bf{h}", align_bytes=64)
            dst = msgs_bf[:].rearrange("p (c i) r -> p c r i", i=4)
            src = msgs_raw[:, :, cols].rearrange("p r (c i) -> p c r i", i=4)
            if h == 0:
                nc.vector.tensor_copy(dst, src)
            else:
                nc.scalar.copy(dst, src)
            nc.vector.quantize_mx(
                msgs_codes[:, cols].bitcast(FP8X4), msgs_scales[:, cols], msgs_bf[:].rearrange("p e r -> p (e r)")
            )

        faded = [keep.tile([P, M], F32, name="faded0", tag="zq_then_faded", align_bytes=64)]
        faded.extend(keep.tile([P, M], F32, name=f"faded{j}") for j in range(1, PACK))
        for j in range(PACK):
            for c in range(4):
                cols = slice(c * HALF, (c + 1) * HALF)
                nc.gpsimd.tensor_tensor(faded[j][:, cols], olds[j][:, cols], fade_all[:, cols], ALU.mult)

        dl_early = keep.tile([P, PACK, 3 * CHUNK], F32, name="dl_early")
        dl_late = keep.tile([P, PACK, CHUNK], F32, name="dl_late")
        wqs = []

        def weigh(c):
            cols = slice(c * CHUNK, (c + 1) * CHUNK)
            scores = psum.tile([P, PACK, CHUNK], F32, name="scores", bufs=2)
            for r in range(PACK):
                nc.tensor.matmul_mx(
                    scores[:, r, :],
                    lhsT=zq_codes[:, r * P : (r + 1) * P].bitcast(FP8X4),
                    lhsT_scale=zq_scales[:, r * P : (r + 1) * P],
                    rhs=got_words[:, cols].bitcast(FP4X4),
                    rhs_scale=got_bytes[:, cols],
                    start=True,
                    stop=True,
                )
            w = keep.tile([P, CHUNK, PACK], F32, name=f"w{c}")
            nc.scalar.activation(w[:], scores[:].rearrange("p r n -> p n r"), ACT.Sigmoid)
            wq = keep.tile([P, CHUNK, PACK], BF16, name=f"wq{c}", align_bytes=64)
            nc.vector.tensor_tensor(
                wq[:], w[:], qs_ps[:, 1, 0:PACK].unsqueeze(1).to_broadcast([P, CHUNK, PACK]), ALU.mult
            )
            wqs.append(wq)

        def carry(c):
            wq_codes = keep.tile([P, CHUNK], U32, name=f"wq_codes{c}", align_bytes=64)
            wq_scales = keep.tile([P, CHUNK], U8, name=f"wq_scales{c}", align_bytes=64)
            nc.vector.quantize_mx(wq_codes[:].bitcast(FP8X4), wq_scales[:], wqs[c][:].rearrange("p n r -> p (n r)"))
            acc = psum.tile([P, PACK, CHUNK], F32, name="acc", bufs=3)
            for j in range(PACK):
                nc.tensor.matmul_mx(
                    acc[:, j, :],
                    lhsT=msgs_codes[:, j * P : (j + 1) * P].bitcast(FP8X4),
                    lhsT_scale=msgs_scales[:, j * P : (j + 1) * P],
                    rhs=wq_codes[:].bitcast(FP8X4),
                    rhs_scale=wq_scales[:],
                    start=True,
                    stop=True,
                )
            nc.scalar.copy(dl_early[:, :, c * CHUNK : (c + 1) * CHUNK] if c < 3 else dl_late[:], acc[:])

        weigh(0)
        for c in range(1, 4):
            weigh(c)
            carry(c - 1)
        carry(3)

        def place_early(on_vector, j):
            scatter(on_vector, placed[j][:], place_list[:, 0:24], dl_early[:, j, :])

        def place_late(on_vector, j):
            scatter(on_vector, placed[j][:], place_list[:, 24:32], dl_late[:, j, :])

        place_early(True, 2)
        place_late(False, 1)
        place_early(False, 1)
        place_early(True, 0)
        place_late(True, 0)
        place_late(False, 2)
        place_late(False, 3)
        place_early(False, 3)
        for j in (1, 0, 2, 3):
            edges = (0, 512, 1024) if j < 3 else (0, 512, 768, 1024)
            for lo, hi in zip(edges, edges[1:]):
                nc.vector.tensor_tensor(faded[j][:, lo:hi], faded[j][:, lo:hi], placed[j][:, lo:hi], ALU.add)
                nc.sync.dma_start(out[P * j : P * (j + 1), lo:hi], faded[j][:, lo:hi])
